import numpy as np
import ml_dtypes


def mxq(x, axis, fmt="e4m3"):
    dtype, down = {"e4m3": (ml_dtypes.float8_e4m3fn, 7), "e5m2": (ml_dtypes.float8_e5m2, 14)}[fmt]
    v = np.moveaxis(np.asarray(x, np.float32).astype(ml_dtypes.bfloat16).astype(np.float64), axis, -1)
    blocks = v.reshape(v.shape[:-1] + (-1, 32))
    amax = np.abs(blocks).max(-1, keepdims=True)
    byte = np.maximum(np.where(amax > 0, np.frexp(amax)[1] - 1 + 127, 0) - down, 1)
    scale = np.exp2(byte - 127.0)
    codes = (blocks / scale).astype(np.float32).astype(dtype).astype(np.float64)
    return np.moveaxis((codes * scale).reshape(v.shape), -1, axis)


WIDE = False


def mx_kscale(k):
    if not WIDE:
        return np.ones(k)
    levels = np.array([10, -10, 5, -5, 0])
    if k % 512:
        return np.exp2(np.random.permutation(np.resize(levels, k // 32))).repeat(32)
    a = np.empty((k // 512, 16))
    for p in range(k // 512):
        a[p, :8] = np.random.permutation(np.resize(levels, 8))
        for g in range(8):
            far = levels[np.abs(levels - a[p, g]) >= 10]
            a[p, g + 8] = far[np.random.randint(len(far))]
    return np.exp2(a.ravel()).repeat(32)


def f64(x):
    return np.asarray(x).astype(np.float64)


def striped(idx):
    return np.tile(np.asarray(idx).reshape(-1, 16).T, (8, 1)).astype(np.uint16)


def unstriped(offs):
    return offs[:16].T.reshape(-1).astype(np.int64)


B, N, T, D, DV, NQ = 1, 512, 1024, 512, 256, 128
CAP = 2.0


def setup_inputs():
    n = np.random.standard_normal
    idx = np.sort(np.random.permutation(T)[:B * N].reshape(B, N), axis=1).reshape(-1)
    s = mx_kscale(D)[:, None]
    u = np.ones(T)
    u[idx] = mx_kscale(B * N)
    r = np.random.uniform(0.5, 2.0, T)
    k = n((D, T)) / s
    v = n((DV, T)) / (u * r)
    return {
        "qT": (n((B, D, NQ)) * s * (0.60 / np.sqrt(D))).astype(np.float32),
        "kT": k.astype(np.float32),
        "vT": v.astype(np.float32),
        "vs": np.tile(u * r, (128, 1)).astype(np.float32),
        "offs": striped(idx),
    }


def reference(qT, kT, vT, vs, offs):
    idx = unstriped(offs)
    k = f64(kT)
    v = f64(vT)
    pick = lambda x: x[:, idx].reshape(x.shape[0], B, N).transpose(1, 0, 2)
    q = f64(qT)
    score = mxq(q, 1, "e4m3").transpose(0, 2, 1) @ mxq(pick(k), 1, "e4m3")
    score = CAP * np.tanh(score / CAP)
    p = 1.0 / (1.0 + np.exp(-score))
    w = p * pick(f64(vs))[:, :1, :]
    y = mxq(w, 2, "e4m3") @ mxq(pick(v).transpose(0, 2, 1), 1, "e4m3")
    y = y / 16.0
    return y

@@ -1,0 +1,146 @@
+from contextlib import ExitStack
+
+import concourse.mybir as mybir
+from concourse.masks import make_identity
+
+F32 = mybir.dt.float32
+BF16 = mybir.dt.bfloat16
+U32 = mybir.dt.uint32
+U16 = mybir.dt.uint16
+U8 = mybir.dt.uint8
+FP8X4 = mybir.dt.float8_e4m3fn_x4
+TANH = mybir.ActivationFunctionType.Tanh
+COPY = mybir.ActivationFunctionType.Copy
+ADD = mybir.AluOpType.add
+MULT = mybir.AluOpType.mult
+
+P = 128
+PACK = 4
+N, T, D, DV, NQ = 512, 1024, 512, 256, 128
+FLOPS = 2 * NQ * N * D + 2 * NQ * N * DV
+
+
+def tile_attend_x_sigmoid_cap_srt_kernel(tc, qT, kT, vT, vs, offs, out):
+    nc = tc.nc
+    with ExitStack() as ctx:
+        held = ctx.enter_context(tc.tile_pool(name="held", bufs=1))
+        psum = ctx.enter_context(tc.psum_pool(name="psum", bufs=1))
+
+        offsets = held.tile([P, N // 16], U16, name="offsets")
+        nc.sync.dma_start(offsets[:], offs)
+        k_rows = kT.rearrange("(p j) n -> p j n", j=PACK)
+        k_pool = []
+        for j in range(PACK):
+            plane = held.tile([P, T], F32, name=f"k_pool{j}")
+            nc.sync.dma_start(plane[:], k_rows[:, j, :])
+            k_pool.append(plane)
+        q_raw = held.tile([P, PACK, NQ], F32, name="q_raw")
+        nc.sync.dma_start(q_raw[:], qT[0].rearrange("(p j) n -> p j n", j=PACK))
+        vs_pool = held.tile([P, T], F32, name="vs_pool")
+        nc.sync.dma_start(vs_pool[:], vs)
+        v_pool = []
+        for b in range(DV // P):
+            block = held.tile([P, T], F32, name=f"v_pool{b}")
+            nc.sync.dma_start(block[:], vT[b * P : (b + 1) * P, :])
+            v_pool.append(block)
+
+        dummy = held.tile([P, 1], F32, name="dummy")
+        nc.gpsimd.memset(dummy[:], 0.0)
+        nc.scalar.activation(dummy[:], dummy[:], TANH)
+        ident_b = held.tile([P, P], BF16, name="ident_b")
+        make_identity(nc, ident_b[:])
+        ident_f = held.tile([P, P], F32, name="ident_f")
+        make_identity(nc, ident_f[:])
+
+        k_grp = held.tile([P, PACK, P, PACK], BF16, name="k_grp", align_bytes=64)
+        for j in range(PACK):
+            nc.vector.tensor_copy(
+                k_grp[:, :, :, j].rearrange("p t s -> p s t"),
+                k_pool[j][:].indirect(offsets[:]),
+            )
+        q_grp = held.tile([P, NQ, PACK], BF16, name="q_grp", align_bytes=64)
+        nc.scalar.copy(q_grp[:], q_raw[:].rearrange("p j n -> p n j"))
+        q_codes = held.tile([P, NQ], U32, name="q_codes", align_bytes=64)
+        q_scales = held.tile([P, NQ], U8, name="q_scales", align_bytes=64)
+        nc.vector.quantize_mx(
+            out=q_codes[:].bitcast(FP8X4), scales=q_scales[:], in_=q_grp[:].rearrange("p n j -> p (n j)")
+        )
+        k_codes = held.tile([P, PACK, P], U32, name="k_codes", align_bytes=64)
+        k_scales = held.tile([P, PACK, P], U8, name="k_scales", align_bytes=64)
+        th1 = held.tile([P, PACK, NQ], F32, name="th1")
+        th2 = held.tile([P, PACK, NQ], F32, name="th2")
+        for h in range(2):
+            pair = slice(2 * h, 2 * h + 2)
+            nc.vector.quantize_mx(
+                out=k_codes[:, pair, :].rearrange("p t s -> p (t s)").bitcast(FP8X4),
+                scales=k_scales[:, pair, :].rearrange("p t s -> p (t s)"),
+                in_=k_grp[:, pair, :, :].rearrange("p t s j -> p (t s j)"),
+            )
+            score = psum.tile([P, 2, NQ], F32, name=f"score{h}")
+            for u in range(2):
+                nc.tensor.matmul_mx(
+                    out=score[:, u, :],
+                    lhsT=k_codes[:, 2 * h + u, :].bitcast(FP8X4),
+                    lhsT_scale=k_scales[:, 2 * h + u, :],
+                    rhs=q_codes[:].bitcast(FP8X4),
+                    rhs_scale=q_scales[:],
+                    start=True,
+                    stop=True,
+                )
+            nc.scalar.activation(th1[:, pair, :], score[:], TANH, scale=0.5)
+
+        vs_got = held.tile([P, N], F32, name="vs_got")
+        nc.vector.tensor_copy(vs_got[:], vs_pool[:].indirect(offsets[:]))
+        vs_turned = psum.tile([P, PACK, P], F32, name="vs_turned")
+        for t in range(PACK):
+            nc.tensor.transpose(vs_turned[:, t, :], vs_got[:, t : N : PACK], ident_f[:])
+
+        w_grp = held.tile([P, NQ, PACK], BF16, name="w_grp", align_bytes=64)
+        for h in range(2):
+            cols = slice(h * NQ // 2, (h + 1) * NQ // 2)
+            nc.scalar.activation(th2[:, :, cols], th1[:, :, cols], TANH)
+            nc.vector.scalar_tensor_tensor(
+                w_grp[:, cols, :],
+                th2[:, :, cols].rearrange("p t q -> p q t"),
+                1.0,
+                vs_turned[:, :, cols].rearrange("p t q -> p q t"),
+                ADD,
+                MULT,
+            )
+        w_codes = held.tile([P, NQ], U32, name="w_codes", align_bytes=64)
+        w_scales = held.tile([P, NQ], U8, name="w_scales", align_bytes=64)
+        nc.vector.quantize_mx(
+            out=w_codes[:].bitcast(FP8X4), scales=w_scales[:], in_=w_grp[:].rearrange("p n j -> p (n j)")
+        )
+
+        v_codes = held.tile([P, DV], U32, name="v_codes", align_bytes=64)
+        v_scales = held.tile([P, DV], U8, name="v_scales", align_bytes=64)
+        for b in range(DV // P):
+            v_got = held.tile([P, PACK, P], BF16, name=f"v_got{b}")
+            nc.vector.tensor_copy(v_got[:].rearrange("p t s -> p s t"), v_pool[b][:].indirect(offsets[:]))
+            v_turned = psum.tile([P, PACK, P], BF16, name=f"v_turned{b}")
+            for t in range(PACK):
+                nc.tensor.transpose(v_turned[:, t, :], v_got[:, t, :], ident_b[:])
+            v_grp = held.tile([P, P, PACK], BF16, name=f"v_grp{b}", align_bytes=64)
+            if b == 0:
+                nc.scalar.copy(v_grp[:], v_turned[:].rearrange("p t e -> p e t"))
+            else:
+                nc.vector.tensor_copy(v_grp[:], v_turned[:].rearrange("p t e -> p e t"))
+            cols = slice(b * P, (b + 1) * P)
+            nc.vector.quantize_mx(
+                out=v_codes[:, cols].bitcast(FP8X4), scales=v_scales[:, cols], in_=v_grp[:].rearrange("p n j -> p (n j)")
+            )
+
+        y = psum.tile([P, DV], F32, name="y")
+        nc.tensor.matmul_mx(
+            out=y[:],
+            lhsT=w_codes[:].bitcast(FP8X4),
+            lhsT_scale=w_scales[:],
+            rhs=v_codes[:].bitcast(FP8X4),
+            rhs_scale=v_scales[:],
+            start=True,
+            stop=True,
+        )
+        result = held.tile([P, DV], F32, name="result")
+        nc.scalar.activation(result[:], y[:], COPY, scale=1.0 / 32.0)
+        nc.sync.dma_start(out[0], result[:])

@@ -36,13 +36,11 @@ def tile_attend_x_sigmoid_cap_srt_kernel(tc, qT, kT, vT, vs, offs, out):
             k_pool.append(plane)
         q_raw = held.tile([P, PACK, NQ], F32, name="q_raw")
         nc.sync.dma_start(q_raw[:], qT[0].rearrange("(p j) n -> p j n", j=PACK))
+        v_pool = [held.tile([P, T], F32, name=f"v_pool{b}") for b in range(DV // P)]
+        nc.sync.dma_start(v_pool[0][:], vT[0:P, :])
         vs_pool = held.tile([P, T], F32, name="vs_pool")
         nc.sync.dma_start(vs_pool[:], vs)
-        v_pool = []
-        for b in range(DV // P):
-            block = held.tile([P, T], F32, name=f"v_pool{b}")
-            nc.sync.dma_start(block[:], vT[b * P : (b + 1) * P, :])
-            v_pool.append(block)
+        nc.sync.dma_start(v_pool[1][:], vT[P : 2 * P, :])
 
         dummy = held.tile([P, 1], F32, name="dummy")
         nc.gpsimd.memset(dummy[:], 0.0)
@@ -53,11 +51,16 @@ def tile_attend_x_sigmoid_cap_srt_kernel(tc, qT, kT, vT, vs, offs, out):
         make_identity(nc, ident_f[:])
 
         k_grp = held.tile([P, PACK, P, PACK], BF16, name="k_grp", align_bytes=64)
-        for j in range(PACK):
-            nc.vector.tensor_copy(
-                k_grp[:, :, :, j].rearrange("p t s -> p s t"),
-                k_pool[j][:].indirect(offsets[:]),
-            )
+        for u in range(2):
+            k_got = held.tile([P, 2, N], F32, name=f"k_got{u}")
+            for i in range(2):
+                nc.vector.tensor_copy(k_got[:, i, :], k_pool[2 * u + i][:].indirect(offsets[:]))
+            dst = k_grp[:, :, :, 2 * u : 2 * u + 2].rearrange("p t s j -> p s t j")
+            src = k_got[:].rearrange("p j (s t) -> p s t j", t=PACK)
+            if u == 0:
+                nc.scalar.copy(dst, src)
+            else:
+                nc.vector.tensor_copy(dst, src)
         q_grp = held.tile([P, NQ, PACK], BF16, name="q_grp", align_bytes=64)
         nc.scalar.copy(q_grp[:], q_raw[:].rearrange("p j n -> p n j"))
         q_codes = held.tile([P, NQ], U32, name="q_codes", align_bytes=64)
@@ -117,30 +120,38 @@ def tile_attend_x_sigmoid_cap_srt_kernel(tc, qT, kT, vT, vs, offs, out):
         v_scales = held.tile([P, DV], U8, name="v_scales", align_bytes=64)
         for b in range(DV // P):
             v_got = held.tile([P, PACK, P], BF16, name=f"v_got{b}")
-            nc.vector.tensor_copy(v_got[:].rearrange("p t s -> p s t"), v_pool[b][:].indirect(offsets[:]))
+            if b == 0:
+                v_half = held.tile([P, T], BF16, name="v_half")
+                nc.scalar.copy(v_half[:], v_pool[b][:])
+                nc.scalar.activation(v_got[:].rearrange("p t s -> p s t"), v_half[:].indirect(offsets[:]), COPY)
+            else:
+                nc.vector.tensor_copy(v_got[:].rearrange("p t s -> p s t"), v_pool[b][:].indirect(offsets[:]))
             v_turned = psum.tile([P, PACK, P], BF16, name=f"v_turned{b}")
             for t in range(PACK):
                 nc.tensor.transpose(v_turned[:, t, :], v_got[:, t, :], ident_b[:])
             v_grp = held.tile([P, P, PACK], BF16, name=f"v_grp{b}", align_bytes=64)
-            if b == 0:
-                nc.scalar.copy(v_grp[:], v_turned[:].rearrange("p t e -> p e t"))
-            else:
-                nc.vector.tensor_copy(v_grp[:], v_turned[:].rearrange("p t e -> p e t"))
+            nc.scalar.copy(v_grp[:], v_turned[:].rearrange("p t e -> p e t"))
             cols = slice(b * P, (b + 1) * P)
             nc.vector.quantize_mx(
                 out=v_codes[:, cols].bitcast(FP8X4), scales=v_scales[:, cols], in_=v_grp[:].rearrange("p n j -> p (n j)")
             )
 
-        y = psum.tile([P, DV], F32, name="y")
-        nc.tensor.matmul_mx(
-            out=y[:],
-            lhsT=w_codes[:].bitcast(FP8X4),
-            lhsT_scale=w_scales[:],
-            rhs=v_codes[:].bitcast(FP8X4),
-            rhs_scale=v_scales[:],
-            start=True,
-            stop=True,
-        )
-        result = held.tile([P, DV], F32, name="result")
-        nc.scalar.activation(result[:], y[:], COPY, scale=1.0 / 32.0)
-        nc.sync.dma_start(out[0], result[:])
+        for b in range(DV // P):
+            cols = slice(b * P, (b + 1) * P)
+            y = psum.tile([P, P], F32, name=f"y{b}")
+            nc.tensor.matmul_mx(
+                out=y[:],
+                lhsT=w_codes[:].bitcast(FP8X4),
+                lhsT_scale=w_scales[:],
+                rhs=v_codes[:, cols].bitcast(FP8X4),
+                rhs_scale=v_scales[:, cols],
+                start=True,
+                stop=True,
+            )
+            result = held.tile([P, P], F32, name=f"result{b}")
+            if b == 0:
+                nc.vector.tensor_scalar(result[:], y[:], 1.0 / 32.0, None, MULT)
+                nc.sync.dma_start(out[0, :, cols], result[:])
+            else:
+                nc.scalar.activation(result[:], y[:], COPY, scale=1.0 / 32.0)
+                nc.scalar.dma_start(out[0, :, cols], result[:])

from contextlib import ExitStack

import concourse.mybir as mybir
from concourse.masks import make_identity

F32 = mybir.dt.float32
BF16 = mybir.dt.bfloat16
U32 = mybir.dt.uint32
U16 = mybir.dt.uint16
U8 = mybir.dt.uint8
FP8X4 = mybir.dt.float8_e4m3fn_x4
TANH = mybir.ActivationFunctionType.Tanh
COPY = mybir.ActivationFunctionType.Copy
ADD = mybir.AluOpType.add
MULT = mybir.AluOpType.mult

P = 128
PACK = 4
N, T, D, DV, NQ = 512, 1024, 512, 256, 128
FLOPS = 2 * NQ * N * D + 2 * NQ * N * DV


def tile_attend_x_sigmoid_cap_srt_kernel(tc, qT, kT, vT, vs, offs, out):
    nc = tc.nc
    with ExitStack() as ctx:
        held = ctx.enter_context(tc.tile_pool(name="held", bufs=1))
        psum = ctx.enter_context(tc.psum_pool(name="psum", bufs=1))

        offsets = held.tile([P, N // 16], U16, name="offsets")
        nc.sync.dma_start(offsets[:], offs)
        k_rows = kT.rearrange("(p j) n -> p j n", j=PACK)
        k_pool = []
        for j in range(PACK):
            plane = held.tile([P, T], F32, name=f"k_pool{j}")
            nc.sync.dma_start(plane[:], k_rows[:, j, :])
            k_pool.append(plane)
        q_raw = held.tile([P, PACK, NQ], F32, name="q_raw")
        nc.sync.dma_start(q_raw[:], qT[0].rearrange("(p j) n -> p j n", j=PACK))
        v_pool = [held.tile([P, T], F32, name=f"v_pool{b}") for b in range(DV // P)]
        nc.sync.dma_start(v_pool[0][:], vT[0:P, :])
        vs_pool = held.tile([P, T], F32, name="vs_pool")
        nc.sync.dma_start(vs_pool[:], vs)
        nc.sync.dma_start(v_pool[1][:], vT[P : 2 * P, :])

        dummy = held.tile([P, 1], F32, name="dummy")
        nc.gpsimd.memset(dummy[:], 0.0)
        nc.scalar.activation(dummy[:], dummy[:], TANH)
        ident_b = held.tile([P, P], BF16, name="ident_b")
        make_identity(nc, ident_b[:])
        ident_f = held.tile([P, P], F32, name="ident_f")
        make_identity(nc, ident_f[:])

        k_grp = held.tile([P, PACK, P, PACK], BF16, name="k_grp", align_bytes=64)
        for u in range(2):
            k_got = held.tile([P, 2, N], F32, name=f"k_got{u}")
            for i in range(2):
                nc.vector.tensor_copy(k_got[:, i, :], k_pool[2 * u + i][:].indirect(offsets[:]))
            dst = k_grp[:, :, :, 2 * u : 2 * u + 2].rearrange("p t s j -> p s t j")
            src = k_got[:].rearrange("p j (s t) -> p s t j", t=PACK)
            if u == 0:
                nc.scalar.copy(dst, src)
            else:
                nc.vector.tensor_copy(dst, src)
        q_grp = held.tile([P, NQ, PACK], BF16, name="q_grp", align_bytes=64)
        nc.scalar.copy(q_grp[:], q_raw[:].rearrange("p j n -> p n j"))
        q_codes = held.tile([P, NQ], U32, name="q_codes", align_bytes=64)
        q_scales = held.tile([P, NQ], U8, name="q_scales", align_bytes=64)
        nc.vector.quantize_mx(
            out=q_codes[:].bitcast(FP8X4), scales=q_scales[:], in_=q_grp[:].rearrange("p n j -> p (n j)")
        )
        k_codes = held.tile([P, PACK, P], U32, name="k_codes", align_bytes=64)
        k_scales = held.tile([P, PACK, P], U8, name="k_scales", align_bytes=64)
        th1 = held.tile([P, PACK, NQ], F32, name="th1")
        th2 = held.tile([P, PACK, NQ], F32, name="th2")
        for h in range(2):
            pair = slice(2 * h, 2 * h + 2)
            nc.vector.quantize_mx(
                out=k_codes[:, pair, :].rearrange("p t s -> p (t s)").bitcast(FP8X4),
                scales=k_scales[:, pair, :].rearrange("p t s -> p (t s)"),
                in_=k_grp[:, pair, :, :].rearrange("p t s j -> p (t s j)"),
            )
            score = psum.tile([P, 2, NQ], F32, name=f"score{h}")
            for u in range(2):
                nc.tensor.matmul_mx(
                    out=score[:, u, :],
                    lhsT=k_codes[:, 2 * h + u, :].bitcast(FP8X4),
                    lhsT_scale=k_scales[:, 2 * h + u, :],
                    rhs=q_codes[:].bitcast(FP8X4),
                    rhs_scale=q_scales[:],
                    start=True,
                    stop=True,
                )
            nc.scalar.activation(th1[:, pair, :], score[:], TANH, scale=0.5)

        vs_got = held.tile([P, N], F32, name="vs_got")
        nc.vector.tensor_copy(vs_got[:], vs_pool[:].indirect(offsets[:]))
        vs_turned = psum.tile([P, PACK, P], F32, name="vs_turned")
        for t in range(PACK):
            nc.tensor.transpose(vs_turned[:, t, :], vs_got[:, t : N : PACK], ident_f[:])

        w_grp = held.tile([P, NQ, PACK], BF16, name="w_grp", align_bytes=64)
        for h in range(2):
            cols = slice(h * NQ // 2, (h + 1) * NQ // 2)
            nc.scalar.activation(th2[:, :, cols], th1[:, :, cols], TANH)
            nc.vector.scalar_tensor_tensor(
                w_grp[:, cols, :],
                th2[:, :, cols].rearrange("p t q -> p q t"),
                1.0,
                vs_turned[:, :, cols].rearrange("p t q -> p q t"),
                ADD,
                MULT,
            )
        w_codes = held.tile([P, NQ], U32, name="w_codes", align_bytes=64)
        w_scales = held.tile([P, NQ], U8, name="w_scales", align_bytes=64)
        nc.vector.quantize_mx(
            out=w_codes[:].bitcast(FP8X4), scales=w_scales[:], in_=w_grp[:].rearrange("p n j -> p (n j)")
        )

        v_codes = held.tile([P, DV], U32, name="v_codes", align_bytes=64)
        v_scales = held.tile([P, DV], U8, name="v_scales", align_bytes=64)
        for b in range(DV // P):
            v_got = held.tile([P, PACK, P], BF16, name=f"v_got{b}")
            if b == 0:
                v_half = held.tile([P, T], BF16, name="v_half")
                nc.scalar.copy(v_half[:], v_pool[b][:])
                nc.scalar.activation(v_got[:].rearrange("p t s -> p s t"), v_half[:].indirect(offsets[:]), COPY)
            else:
                nc.vector.tensor_copy(v_got[:].rearrange("p t s -> p s t"), v_pool[b][:].indirect(offsets[:]))
            v_turned = psum.tile([P, PACK, P], BF16, name=f"v_turned{b}")
            for t in range(PACK):
                nc.tensor.transpose(v_turned[:, t, :], v_got[:, t, :], ident_b[:])
            v_grp = held.tile([P, P, PACK], BF16, name=f"v_grp{b}", align_bytes=64)
            nc.scalar.copy(v_grp[:], v_turned[:].rearrange("p t e -> p e t"))
            cols = slice(b * P, (b + 1) * P)
            nc.vector.quantize_mx(
                out=v_codes[:, cols].bitcast(FP8X4), scales=v_scales[:, cols], in_=v_grp[:].rearrange("p n j -> p (n j)")
            )

        for b in range(DV // P):
            cols = slice(b * P, (b + 1) * P)
            y = psum.tile([P, P], F32, name=f"y{b}")
            nc.tensor.matmul_mx(
                out=y[:],
                lhsT=w_codes[:].bitcast(FP8X4),
                lhsT_scale=w_scales[:],
                rhs=v_codes[:, cols].bitcast(FP8X4),
                rhs_scale=v_scales[:, cols],
                start=True,
                stop=True,
            )
            result = held.tile([P, P], F32, name=f"result{b}")
            if b == 0:
                nc.vector.tensor_scalar(result[:], y[:], 1.0 / 32.0, None, MULT)
                nc.sync.dma_start(out[0, :, cols], result[:])
            else:
                nc.scalar.activation(result[:], y[:], COPY, scale=1.0 / 32.0)
                nc.scalar.dma_start(out[0, :, cols], result[:])
